import numpy as np
import ml_dtypes


def mxq(x, axis, fmt="e4m3"):
    dtype, down = {"e4m3": (ml_dtypes.float8_e4m3fn, 7), "e5m2": (ml_dtypes.float8_e5m2, 14)}[fmt]
    v = np.moveaxis(np.asarray(x, np.float32).astype(ml_dtypes.bfloat16).astype(np.float64), axis, -1)
    blocks = v.reshape(v.shape[:-1] + (-1, 32))
    amax = np.abs(blocks).max(-1, keepdims=True)
    byte = np.maximum(np.where(amax > 0, np.frexp(amax)[1] - 1 + 127, 0) - down, 1)
    scale = np.exp2(byte - 127.0)
    codes = (blocks / scale).astype(np.float32).astype(dtype).astype(np.float64)
    return np.moveaxis((codes * scale).reshape(v.shape), -1, axis)


WIDE = False


def mx_kscale(k):
    if not WIDE:
        return np.ones(k)
    levels = np.array([10, -10, 5, -5, 0])
    if k % 512:
        return np.exp2(np.random.permutation(np.resize(levels, k // 32))).repeat(32)
    a = np.empty((k // 512, 16))
    for p in range(k // 512):
        a[p, :8] = np.random.permutation(np.resize(levels, 8))
        for g in range(8):
            far = levels[np.abs(levels - a[p, g]) >= 10]
            a[p, g + 8] = far[np.random.randint(len(far))]
    return np.exp2(a.ravel()).repeat(32)


def f64(x):
    return np.asarray(x).astype(np.float64)


def striped(idx):
    return np.tile(np.asarray(idx).reshape(-1, 16).T, (8, 1)).astype(np.uint16)


def unstriped(offs):
    return offs[:16].T.reshape(-1).astype(np.int64)


E2M1 = np.array([0.0, 0.5, 1.0, 1.5, 2.0, 3.0, 4.0, 6.0, -0.0, -0.5, -1.0, -1.5, -2.0, -3.0, -4.0, -6.0])


def pack_weight(w, fmt):
    k, n = w.shape
    w = f64(np.asarray(w, np.float32).astype(ml_dtypes.bfloat16)).reshape(k // 32, 32, n)
    amax = np.abs(w).max(1)
    if fmt == "e4m3":
        byte = np.frexp(amax)[1] - 1 + 127 - 7
    else:
        mant, ex = np.frexp(amax / 6.0)
        byte = np.where(mant > 0.5, ex, ex - 1) + 127
    byte = np.clip(np.where(amax > 0, byte, 1), 1, 254)
    scaled = (w * np.exp2(127.0 - byte)[:, None, :]).reshape(k, n).astype(np.float32)
    by_word = np.ascontiguousarray(scaled.reshape(k // 512, 128, 4, n).transpose(0, 1, 3, 2))
    if fmt == "e4m3":
        words = by_word.astype(ml_dtypes.float8_e4m3fn).view(np.uint8)
    else:
        c = by_word.astype(ml_dtypes.float4_e2m1fn).view(np.uint8) & 0xF
        words = (c[..., 0::2] | (c[..., 1::2] << 4)).reshape(k // 512, 128, 2 * n)
    return np.ascontiguousarray(words), np.ascontiguousarray(byte.astype(np.uint8).reshape(k // 512, 16, n))


def unpack_weight(words, scales, fmt):
    g, _, n = scales.shape
    words = np.ascontiguousarray(words).reshape(g, 128, n, -1)
    if fmt == "e4m3":
        vals = words.view(ml_dtypes.float8_e4m3fn).astype(np.float64)
    else:
        nib = np.empty((g, 128, n, 4), np.uint8)
        nib[..., 0::2] = words & 0xF
        nib[..., 1::2] = words >> 4
        vals = E2M1[nib]
    vals = vals * np.repeat(np.exp2(scales.astype(np.float64) - 127.0), 8, axis=1)[..., None]
    return vals.transpose(0, 1, 3, 2).reshape(g * 512, n)


D, K, R, T, I, Q, G = 512, 512, 512, 2048, 512, 128, 32


def setup_inputs():
    n = np.random.standard_normal
    idx = np.random.permutation(T)[:I]
    fd = mx_kscale(D)
    fk = mx_kscale(K)
    fr = mx_kscale(R)
    keysp = pack_weight(n((D, T)) / fd[:, None], "e2m1")
    tabp = pack_weight(n((K, T)) / fk[:, None], "e2m1")
    return {
        "query": (n((D, Q)) * 0.7 / np.sqrt(D) * fd[:, None]).astype(np.float32),
        "keys_words": keysp[0],
        "keys_scales": keysp[1],
        "tab_words": tabp[0],
        "tab_scales": tabp[1],
        "w1": (n((K, R)) * 1 / np.sqrt(K) * fk[:, None]).astype(np.float32),
        "share": (np.random.uniform(0.4, 1.0, (R, 1))).astype(np.float32),
        "gout": (n((R, Q)) * 1 / np.sqrt(R) * fr[:, None]).astype(np.float32),
        "hsc": (np.random.uniform(0.7, 1.4, (R, 1)) / fr[:, None]).astype(np.float32),
        "old": (0.5 * n((Q, T))).astype(np.float32),
        "offs": striped(idx),
    }


def reference(query, keys_words, keys_scales, tab_words, tab_scales, w1, share, gout, hsc, old, offs):
    idx = unstriped(offs)
    keysu = unpack_weight(keys_words, keys_scales, "e2m1")
    tabu = unpack_weight(tab_words, tab_scales, "e2m1")
    queryq = mxq(f64(query), 0, "e4m3")
    keysidxg = keysu[:, idx]
    a = queryq.T @ keysidxg
    p = np.exp(a - np.max(a, axis=1, keepdims=True))
    z = np.sum(p, axis=1, keepdims=True)
    w1q = mxq(f64(w1), 0, "e4m3")
    tabidxg = tabu[:, idx]
    zh = w1q.T @ tabidxg
    mz = zh.reshape(R, G, I // G).mean(axis=2)
    mzr = np.repeat(mz, I // G, axis=1)
    hv = np.tanh(zh - mzr * f64(share))
    hs1 = hv * f64(hsc)
    goutq = mxq(f64(gout), 0, "e4m3")
    hs1q = mxq(hs1, 0, "e4m3")
    c0 = goutq.T @ hs1q
    dz = np.sum(c0 * p / np.square(z) * (-1.0), axis=1, keepdims=True)
    dp = c0 / z + dz
    da = dp * p
    gs = da * 512.0
    gf = np.zeros((Q, T))
    gf[:, idx] = gs
    y = f64(old) + gf
    return y

@@ -1,0 +1,216 @@
+from contextlib import ExitStack
+
+import concourse.mybir as mybir
+
+F32 = mybir.dt.float32
+BF16 = mybir.dt.bfloat16
+I32 = mybir.dt.int32
+U32 = mybir.dt.uint32
+U16 = mybir.dt.uint16
+U8 = mybir.dt.uint8
+FP8X4 = mybir.dt.float8_e4m3fn_x4
+FP4X4 = mybir.dt.float4_e2m1fn_x4
+ALU = mybir.AluOpType
+ACT = mybir.ActivationFunctionType
+AX = mybir.AxisListType
+
+P = 128
+PACK = 4
+R, T, SLOTS, Q = 512, 2048, 512, 128
+PAGE = 16
+CHUNK = 128
+CHUNKS = SLOTS // CHUNK
+PAGES = CHUNK // PAGE
+OUT_CHUNK = 512
+
+FLOPS = 2 * 512 * SLOTS * (Q + R + Q)
+
+
+def tile_attend_blrcentred_soft_kernel(tc, query, keys_words, keys_scales, tab_words, tab_scales,
+                                        w1, share, gout, hsc, old, offs, out):
+    nc = tc.nc
+    with ExitStack() as ctx:
+        keep = ctx.enter_context(tc.tile_pool(name="keep", bufs=1))
+        psum = ctx.enter_context(tc.psum_pool(name="psum", bufs=1))
+
+        def sb(name, shape, dtype):
+            return keep.tile(shape, dtype, name=name, align_bytes=64)
+
+        offsets = keep.tile([P, SLOTS // 16], U16, name="offsets")
+        tab_w = sb("tab_w", [P, T], U16)
+        tab_s = sb("tab_s", [P, T], U8)
+        keys_w = sb("keys_w", [P, T], U16)
+        keys_s = sb("keys_s", [P, T], U8)
+        gf = sb("gf", [P, T], F32)
+        warm = sb("warm", [P, 1], F32)
+        warm2 = sb("warm2", [P, 1], F32)
+
+        nc.vector.memset(tab_s[:].bitcast(I32), 0)
+        nc.vector.memset(keys_s[:].bitcast(I32), 0)
+        nc.gpsimd.memset(warm[:], 0.0)
+        nc.scalar.activation(out=warm2[:], in_=warm[:], func=ACT.Exp)
+        nc.vector.memset(gf[:], 0.0)
+
+        def load_words(tile, words):
+            nc.sync.dma_start(out=tile[:].bitcast(I32), in_=words[0].bitcast(I32))
+
+        def load_scales(tile, scales):
+            for quad in range(4):
+                nc.sync.dma_start(out=tile[32 * quad : 32 * quad + 4, :].bitcast(I32),
+                                  in_=scales[0, 4 * quad : 4 * quad + 4, :].bitcast(I32))
+
+        nc.sync.dma_start(offsets[:], offs)
+        load_words(tab_w, tab_words)
+        load_scales(tab_s, tab_scales)
+        w_rows = w1.rearrange("(p j) c -> p j c", j=PACK)
+        w_raw = []
+        for h in range(2):
+            half = sb("w_raw%d" % h, [P, PACK, R // 2], F32)
+            nc.sync.dma_start(out=half[:], in_=w_rows[:, :, h * (R // 2) : (h + 1) * (R // 2)])
+            w_raw.append(half)
+        load_words(keys_w, keys_words)
+        load_scales(keys_s, keys_scales)
+        share_sb = sb("share_sb", [P, PACK], F32)
+        nc.sync.dma_start(out=share_sb[:], in_=share.rearrange("(p t) o -> p (t o)", t=PACK))
+        hsc_sb = sb("hsc_sb", [P, PACK], F32)
+        nc.sync.dma_start(out=hsc_sb[:], in_=hsc.rearrange("(p t) o -> p (t o)", t=PACK))
+        q_raw = sb("q_raw", [P, PACK, Q], F32)
+        nc.sync.dma_start(out=q_raw[:], in_=query.rearrange("(p j) c -> p j c", j=PACK))
+        g_raw = sb("g_raw", [P, PACK, Q], F32)
+        nc.sync.dma_start(out=g_raw[:], in_=gout.rearrange("(p j) c -> p j c", j=PACK))
+        old_sb = sb("old_sb", [P, T], F32)
+        nc.sync.dma_start(out=old_sb[:], in_=old)
+
+        def gather(name, window, dtype):
+            got = sb(name, [P, SLOTS], dtype)
+            nc.vector.tensor_copy(out=got[:], in_=window[:].indirect(offsets[:]))
+            return got
+
+        tab_wg = gather("tab_wg", tab_w, U16)
+        tab_sg = gather("tab_sg", tab_s, U8)
+
+        w_bf = sb("w_bf", [P, PACK, P, PACK], BF16)
+        for h in range(2):
+            nc.scalar.copy(
+                out=w_bf[:, :, h * 64 : (h + 1) * 64, :].rearrange("p t m j -> p m j t"),
+                in_=w_raw[h][:].rearrange("p j (m t) -> p m j t", t=PACK))
+        w_codes = sb("w_codes", [P, R], U32)
+        w_scales = sb("w_scales", [P, R], U8)
+        nc.vector.quantize_mx(out=w_codes[:].bitcast(FP8X4), scales=w_scales[:],
+                              in_=w_bf[:].rearrange("p t m j -> p (t m j)"))
+
+        qg_bf = sb("qg_bf", [P, 2, Q, PACK], BF16)
+        for n, raw in enumerate((q_raw, g_raw)):
+            nc.scalar.copy(
+                out=qg_bf[:, n, :, :].rearrange("p (c i) j -> p c j i", i=4),
+                in_=raw[:].rearrange("p j (c i) -> p c j i", i=4))
+
+        zh = []
+        for c in range(CHUNKS):
+            bank = psum.tile([P, PACK, CHUNK], F32, name="zh%d" % c)
+            cols = slice(c * CHUNK, (c + 1) * CHUNK)
+            for t in range(PACK):
+                nc.tensor.matmul_mx(
+                    out=bank[:, t, :],
+                    lhsT=w_codes[:, t * P : (t + 1) * P].bitcast(FP8X4),
+                    lhsT_scale=w_scales[:, t * P : (t + 1) * P],
+                    rhs=tab_wg[:, cols].bitcast(FP4X4), rhs_scale=tab_sg[:, cols],
+                    start=True, stop=True)
+            zh.append(bank)
+
+        sums = [sb("sums%d" % n, [P, 2, PACK, PAGES], F32) for n in range(2)]
+        shift = [sb("shift%d" % n, [P, 2, PACK, PAGES], F32) for n in range(2)]
+        hs_bf = sb("hs_bf", [P, SLOTS, PACK], BF16)
+        hs_codes = sb("hs_codes", [P, SLOTS], U32)
+        hs_scales = sb("hs_scales", [P, SLOTS], U8)
+        hv = {}
+
+        def page_sums(c):
+            nc.vector.tensor_reduce(
+                out=sums[c // 2][:, c % 2, :, :].rearrange("p t g -> p (t g)"),
+                in_=zh[c][:].rearrange("p t (g s) -> p (t g) s", s=PAGE), axis=AX.X, op=ALU.add)
+
+        def page_shift(n):
+            nc.vector.tensor_tensor(
+                out=shift[n][:], in0=sums[n][:],
+                in1=share16[:].unsqueeze(1).unsqueeze(3).to_broadcast([P, 2, PACK, PAGES]), op=ALU.mult)
+
+        def centre(c):
+            x = sb("x%d" % c, [P, CHUNK, PACK], F32)
+            nc.vector.tensor_tensor(
+                out=x[:].rearrange("p (g s) t -> p g s t", s=PAGE),
+                in0=zh[c][:].rearrange("p t (g s) -> p g s t", s=PAGE),
+                in1=shift[c // 2][:, c % 2, :, :].rearrange("p t g -> p g t").unsqueeze(2).to_broadcast([P, PAGES, PAGE, PACK]),
+                op=ALU.subtract)
+            hv[c] = sb("hv%d" % c, [P, CHUNK, PACK], F32)
+            nc.scalar.activation(out=hv[c][:], in_=x[:], func=ACT.Tanh)
+
+        def scale(c):
+            nc.vector.tensor_tensor(
+                out=hs_bf[:, c * CHUNK : (c + 1) * CHUNK, :], in0=hv[c][:],
+                in1=hsc_sb[:].unsqueeze(1).to_broadcast([P, CHUNK, PACK]), op=ALU.mult)
+
+        c0 = psum.tile([P, SLOTS], F32, name="c0")
+
+        def second_product(n):
+            cols = slice(2 * n * CHUNK, 2 * (n + 1) * CHUNK)
+            nc.vector.quantize_mx(out=hs_codes[:, cols].bitcast(FP8X4), scales=hs_scales[:, cols],
+                                  in_=hs_bf[:, cols, :].rearrange("p i t -> p (i t)"))
+            nc.tensor.matmul_mx(out=c0[:, cols], lhsT=qg_codes[:, Q:].bitcast(FP8X4), lhsT_scale=qg_scales[:, Q:],
+                                rhs=hs_codes[:, cols].bitcast(FP8X4), rhs_scale=hs_scales[:, cols],
+                                start=True, stop=True)
+
+        share16 = sb("share16", [P, PACK], F32)
+        nc.scalar.mul(out=share16[:], in_=share_sb[:], mul=1.0 / PAGE)
+
+        keys_wg = gather("keys_wg", keys_w, U16)
+        page_sums(0)
+        page_sums(1)
+        keys_sg = gather("keys_sg", keys_s, U8)
+        page_shift(0)
+        qg_codes = sb("qg_codes", [P, 2 * Q], U32)
+        qg_scales = sb("qg_scales", [P, 2 * Q], U8)
+        nc.vector.quantize_mx(out=qg_codes[:].bitcast(FP8X4), scales=qg_scales[:],
+                              in_=qg_bf[:].rearrange("p n c j -> p (n c j)"))
+        a = psum.tile([P, SLOTS], F32, name="a")
+        nc.tensor.matmul_mx(out=a[:], lhsT=qg_codes[:, :Q].bitcast(FP8X4), lhsT_scale=qg_scales[:, :Q],
+                            rhs=keys_wg[:].bitcast(FP4X4), rhs_scale=keys_sg[:], start=True, stop=True)
+        centre(0)
+        centre(1)
+        page_sums(2)
+        page_sums(3)
+        neg_max = sb("neg_max", [P, 1], F32)
+        nc.vector.tensor_reduce(out=neg_max[:], in_=a[:], axis=AX.X, op=ALU.max, negate=True)
+        p = sb("p", [P, SLOTS], F32)
+        z = sb("z", [P, 1], F32)
+        nc.scalar.activation(out=p[:], in_=a[:], func=ACT.Exp, bias=neg_max[:], accum_out=z[:])
+        page_shift(1)
+        scale(0)
+        centre(2)
+        scale(1)
+        centre(3)
+        second_product(0)
+        rz = sb("rz", [P, 1], F32)
+        nc.vector.reciprocal(out=rz[:], in_=z[:])
+        rz_gain = sb("rz_gain", [P, 1], F32)
+        nc.scalar.mul(out=rz_gain[:], in_=rz[:], mul=512.0)
+        rz_neg = sb("rz_neg", [P, 1], F32)
+        nc.scalar.mul(out=rz_neg[:], in_=rz[:], mul=-1.0)
+        scale(2)
+        scale(3)
+        second_product(1)
+
+        u = sb("u", [P, SLOTS], F32)
+        total = sb("total", [P, 1], F32)
+        nc.vector.scalar_tensor_tensor(out=u[:], in0=c0[:], scalar=rz_gain[:], in1=p[:],
+                                       op0=ALU.mult, op1=ALU.mult, accum_out=total[:])
+        w = sb("w", [P, SLOTS], F32)
+        nc.vector.tensor_scalar(out=w[:], in0=p[:], scalar1=total[:], scalar2=rz_neg[:], op0=ALU.mult, op1=ALU.mult)
+        nc.vector.tensor_tensor(out=gf[:].indirect(offsets[:]), in0=u[:], in1=w[:], op=ALU.add)
+
+        for n in range(T // OUT_CHUNK):
+            cols = slice(n * OUT_CHUNK, (n + 1) * OUT_CHUNK)
+            y = sb("y%d" % n, [P, OUT_CHUNK], F32)
+            nc.vector.tensor_tensor(out=y[:], in0=gf[:, cols], in1=old_sb[:, cols], op=ALU.add)
+            queue = nc.sync if n % 2 == 0 else nc.scalar
+            queue.dma_start(out=out[:, cols], in_=y[:])

@@ -71,9 +71,9 @@ def tile_attend_blrcentred_soft_kernel(tc, query, keys_words, keys_scales, tab_w
         load_words(keys_w, keys_words)
         load_scales(keys_s, keys_scales)
         share_sb = sb("share_sb", [P, PACK], F32)
-        nc.sync.dma_start(out=share_sb[:], in_=share.rearrange("(p t) o -> p (t o)", t=PACK))
+        nc.gpsimd.dma_start(out=share_sb[:], in_=share.rearrange("(p t) o -> p (t o)", t=PACK))
         hsc_sb = sb("hsc_sb", [P, PACK], F32)
-        nc.sync.dma_start(out=hsc_sb[:], in_=hsc.rearrange("(p t) o -> p (t o)", t=PACK))
+        nc.gpsimd.dma_start(out=hsc_sb[:], in_=hsc.rearrange("(p t) o -> p (t o)", t=PACK))
         q_raw = sb("q_raw", [P, PACK, Q], F32)
         nc.sync.dma_start(out=q_raw[:], in_=query.rearrange("(p j) c -> p j c", j=PACK))
         g_raw = sb("g_raw", [P, PACK, Q], F32)
@@ -90,10 +90,9 @@ def tile_attend_blrcentred_soft_kernel(tc, query, keys_words, keys_scales, tab_w
         tab_sg = gather("tab_sg", tab_s, U8)
 
         w_bf = sb("w_bf", [P, PACK, P, PACK], BF16)
-        for h in range(2):
-            nc.scalar.copy(
-                out=w_bf[:, :, h * 64 : (h + 1) * 64, :].rearrange("p t m j -> p m j t"),
-                in_=w_raw[h][:].rearrange("p j (m t) -> p m j t", t=PACK))
+        for copy, h, lo, hi in ((nc.scalar.copy, 0, 0, 64), (nc.scalar.copy, 1, 0, 24), (nc.vector.tensor_copy, 1, 24, 64)):
+            copy(out=w_bf[:, :, h * 64 + lo : h * 64 + hi, :].rearrange("p t m j -> p m j t"),
+                 in_=w_raw[h][:].rearrange("p j (m t) -> p m j t", t=PACK)[:, lo:hi, :, :])
         w_codes = sb("w_codes", [P, R], U32)
         w_scales = sb("w_scales", [P, R], U8)
         nc.vector.quantize_mx(out=w_codes[:].bitcast(FP8X4), scales=w_scales[:],
@@ -118,36 +117,26 @@ def tile_attend_blrcentred_soft_kernel(tc, query, keys_words, keys_scales, tab_w
                     start=True, stop=True)
             zh.append(bank)
 
-        sums = [sb("sums%d" % n, [P, 2, PACK, PAGES], F32) for n in range(2)]
-        shift = [sb("shift%d" % n, [P, 2, PACK, PAGES], F32) for n in range(2)]
-        hs_bf = sb("hs_bf", [P, SLOTS, PACK], BF16)
+        sums = sb("sums", [P, PACK, CHUNKS, PAGES], F32)
+        shift = keep.tile([P, PACK, CHUNKS, PAGES], F32, name="shift", tag="shift", align_bytes=64)
+        hs_bf = [sb("hs_bf%d" % n, [P, 2, CHUNK, PACK], BF16) for n in range(2)]
         hs_codes = sb("hs_codes", [P, SLOTS], U32)
         hs_scales = sb("hs_scales", [P, SLOTS], U8)
         hv = {}
-
-        def page_sums(c):
-            nc.vector.tensor_reduce(
-                out=sums[c // 2][:, c % 2, :, :].rearrange("p t g -> p (t g)"),
-                in_=zh[c][:].rearrange("p t (g s) -> p (t g) s", s=PAGE), axis=AX.X, op=ALU.add)
-
-        def page_shift(n):
-            nc.vector.tensor_tensor(
-                out=shift[n][:], in0=sums[n][:],
-                in1=share16[:].unsqueeze(1).unsqueeze(3).to_broadcast([P, 2, PACK, PAGES]), op=ALU.mult)
 
         def centre(c):
             x = sb("x%d" % c, [P, CHUNK, PACK], F32)
             nc.vector.tensor_tensor(
                 out=x[:].rearrange("p (g s) t -> p g s t", s=PAGE),
                 in0=zh[c][:].rearrange("p t (g s) -> p g s t", s=PAGE),
-                in1=shift[c // 2][:, c % 2, :, :].rearrange("p t g -> p g t").unsqueeze(2).to_broadcast([P, PAGES, PAGE, PACK]),
+                in1=shift[:, :, c, :].rearrange("p t g -> p g t").unsqueeze(2).to_broadcast([P, PAGES, PAGE, PACK]),
                 op=ALU.subtract)
             hv[c] = sb("hv%d" % c, [P, CHUNK, PACK], F32)
             nc.scalar.activation(out=hv[c][:], in_=x[:], func=ACT.Tanh)
 
-        def scale(c):
-            nc.vector.tensor_tensor(
-                out=hs_bf[:, c * CHUNK : (c + 1) * CHUNK, :], in0=hv[c][:],
+        def scale(engine, c):
+            engine.tensor_tensor(
+                out=hs_bf[c // 2][:, c % 2, :, :], in0=hv[c][:],
                 in1=hsc_sb[:].unsqueeze(1).to_broadcast([P, CHUNK, PACK]), op=ALU.mult)
 
         c0 = psum.tile([P, SLOTS], F32, name="c0")
@@ -155,50 +144,49 @@ def tile_attend_blrcentred_soft_kernel(tc, query, keys_words, keys_scales, tab_w
         def second_product(n):
             cols = slice(2 * n * CHUNK, 2 * (n + 1) * CHUNK)
             nc.vector.quantize_mx(out=hs_codes[:, cols].bitcast(FP8X4), scales=hs_scales[:, cols],
-                                  in_=hs_bf[:, cols, :].rearrange("p i t -> p (i t)"))
+                                  in_=hs_bf[n][:].rearrange("p c i t -> p (c i t)"))
             nc.tensor.matmul_mx(out=c0[:, cols], lhsT=qg_codes[:, Q:].bitcast(FP8X4), lhsT_scale=qg_scales[:, Q:],
                                 rhs=hs_codes[:, cols].bitcast(FP8X4), rhs_scale=hs_scales[:, cols],
                                 start=True, stop=True)
 
-        share16 = sb("share16", [P, PACK], F32)
-        nc.scalar.mul(out=share16[:], in_=share_sb[:], mul=1.0 / PAGE)
 
         keys_wg = gather("keys_wg", keys_w, U16)
-        page_sums(0)
-        page_sums(1)
-        keys_sg = gather("keys_sg", keys_s, U8)
-        page_shift(0)
+        for c in range(CHUNKS):
+            nc.vector.tensor_reduce(
+                out=sums[:, :, c, :],
+                in_=zh[c][:].rearrange("p t (g s) -> p t g s", s=PAGE), axis=AX.X, op=ALU.add)
         qg_codes = sb("qg_codes", [P, 2 * Q], U32)
         qg_scales = sb("qg_scales", [P, 2 * Q], U8)
+        nc.vector.scalar_tensor_tensor(
+            out=shift[:].rearrange("p t c g -> p t (c g)"), in0=sums[:].rearrange("p t c g -> p t (c g)"),
+            scalar=1.0 / PAGE, in1=share_sb[:].unsqueeze(2).to_broadcast([P, PACK, CHUNKS * PAGES]),
+            op0=ALU.mult, op1=ALU.mult)
         nc.vector.quantize_mx(out=qg_codes[:].bitcast(FP8X4), scales=qg_scales[:],
                               in_=qg_bf[:].rearrange("p n c j -> p (n c j)"))
+        for c in range(CHUNKS):
+            centre(c)
+        scale(nc.gpsimd, 0)
+        scale(nc.gpsimd, 1)
+        keys_sg = keep.tile([P, SLOTS], U8, name="keys_sg", tag="shift", align_bytes=64)
+        nc.vector.tensor_copy(out=keys_sg[:], in_=keys_s[:].indirect(offsets[:]))
         a = psum.tile([P, SLOTS], F32, name="a")
         nc.tensor.matmul_mx(out=a[:], lhsT=qg_codes[:, :Q].bitcast(FP8X4), lhsT_scale=qg_scales[:, :Q],
                             rhs=keys_wg[:].bitcast(FP4X4), rhs_scale=keys_sg[:], start=True, stop=True)
-        centre(0)
-        centre(1)
-        page_sums(2)
-        page_sums(3)
+        scale(nc.vector, 2)
         neg_max = sb("neg_max", [P, 1], F32)
         nc.vector.tensor_reduce(out=neg_max[:], in_=a[:], axis=AX.X, op=ALU.max, negate=True)
         p = sb("p", [P, SLOTS], F32)
         z = sb("z", [P, 1], F32)
         nc.scalar.activation(out=p[:], in_=a[:], func=ACT.Exp, bias=neg_max[:], accum_out=z[:])
-        page_shift(1)
-        scale(0)
-        centre(2)
-        scale(1)
-        centre(3)
+        scale(nc.vector, 3)
         second_product(0)
+        second_product(1)
         rz = sb("rz", [P, 1], F32)
         nc.vector.reciprocal(out=rz[:], in_=z[:])
         rz_gain = sb("rz_gain", [P, 1], F32)
-        nc.scalar.mul(out=rz_gain[:], in_=rz[:], mul=512.0)
+        nc.vector.tensor_scalar_mul(out=rz_gain[:], in0=rz[:], scalar1=512.0)
         rz_neg = sb("rz_neg", [P, 1], F32)
-        nc.scalar.mul(out=rz_neg[:], in_=rz[:], mul=-1.0)
-        scale(2)
-        scale(3)
-        second_product(1)
+        nc.vector.tensor_scalar_mul(out=rz_neg[:], in0=rz[:], scalar1=-1.0)
 
         u = sb("u", [P, SLOTS], F32)
         total = sb("total", [P, 1], F32)
@@ -208,9 +196,10 @@ def tile_attend_blrcentred_soft_kernel(tc, query, keys_words, keys_scales, tab_w
         nc.vector.tensor_scalar(out=w[:], in0=p[:], scalar1=total[:], scalar2=rz_neg[:], op0=ALU.mult, op1=ALU.mult)
         nc.vector.tensor_tensor(out=gf[:].indirect(offsets[:]), in0=u[:], in1=w[:], op=ALU.add)
 
-        for n in range(T // OUT_CHUNK):
-            cols = slice(n * OUT_CHUNK, (n + 1) * OUT_CHUNK)
-            y = sb("y%d" % n, [P, OUT_CHUNK], F32)
+        edges = (0, 256, 768, 1280, 1792, 2048)
+        for n in range(len(edges) - 1):
+            cols = slice(edges[n], edges[n + 1])
+            y = sb("y%d" % n, [P, edges[n + 1] - edges[n]], F32)
             nc.vector.tensor_tensor(out=y[:], in0=gf[:, cols], in1=old_sb[:, cols], op=ALU.add)
             queue = nc.sync if n % 2 == 0 else nc.scalar
             queue.dma_start(out=out[:, cols], in_=y[:])

@@ -55,9 +55,8 @@ def tile_attend_blrcentred_soft_kernel(tc, query, keys_words, keys_scales, tab_w
             nc.sync.dma_start(out=tile[:].bitcast(I32), in_=words[0].bitcast(I32))
 
         def load_scales(tile, scales):
-            for quad in range(4):
-                nc.sync.dma_start(out=tile[32 * quad : 32 * quad + 4, :].bitcast(I32),
-                                  in_=scales[0, 4 * quad : 4 * quad + 4, :].bitcast(I32))
+            for f in range(4):
+                nc.sync.dma_start(out=tile[f : P : 32, :].bitcast(I32), in_=scales[0, f : 16 : 4, :].bitcast(I32))
 
         nc.sync.dma_start(offsets[:], offs)
         load_words(tab_w, tab_words)
@@ -117,8 +116,8 @@ def tile_attend_blrcentred_soft_kernel(tc, query, keys_words, keys_scales, tab_w
                     start=True, stop=True)
             zh.append(bank)
 
-        sums = sb("sums", [P, PACK, CHUNKS, PAGES], F32)
-        shift = keep.tile([P, PACK, CHUNKS, PAGES], F32, name="shift", tag="shift", align_bytes=64)
+        sums = keep.tile([P, CHUNKS, PAGES, PACK], F32, name="sums", tag="sums", align_bytes=64)
+        shift = sb("shift", [P, CHUNKS, PAGES, PACK], F32)
         hs_bf = [sb("hs_bf%d" % n, [P, 2, CHUNK, PACK], BF16) for n in range(2)]
         hs_codes = sb("hs_codes", [P, SLOTS], U32)
         hs_scales = sb("hs_scales", [P, SLOTS], U8)
@@ -129,15 +128,15 @@ def tile_attend_blrcentred_soft_kernel(tc, query, keys_words, keys_scales, tab_w
             nc.vector.tensor_tensor(
                 out=x[:].rearrange("p (g s) t -> p g s t", s=PAGE),
                 in0=zh[c][:].rearrange("p t (g s) -> p g s t", s=PAGE),
-                in1=shift[:, :, c, :].rearrange("p t g -> p g t").unsqueeze(2).to_broadcast([P, PAGES, PAGE, PACK]),
+                in1=shift[:, c, :, :].unsqueeze(2).to_broadcast([P, PAGES, PAGE, PACK]),
                 op=ALU.subtract)
             hv[c] = sb("hv%d" % c, [P, CHUNK, PACK], F32)
             nc.scalar.activation(out=hv[c][:], in_=x[:], func=ACT.Tanh)
 
-        def scale(engine, c):
+        def scale(engine, c, lo, hi):
             engine.tensor_tensor(
-                out=hs_bf[c // 2][:, c % 2, :, :], in0=hv[c][:],
-                in1=hsc_sb[:].unsqueeze(1).to_broadcast([P, CHUNK, PACK]), op=ALU.mult)
+                out=hs_bf[c // 2][:, c % 2, lo:hi, :], in0=hv[c][:, lo:hi, :],
+                in1=hsc_sb[:].unsqueeze(1).to_broadcast([P, hi - lo, PACK]), op=ALU.mult)
 
         c0 = psum.tile([P, SLOTS], F32, name="c0")
 
@@ -153,47 +152,47 @@ def tile_attend_blrcentred_soft_kernel(tc, query, keys_words, keys_scales, tab_w
         keys_wg = gather("keys_wg", keys_w, U16)
         for c in range(CHUNKS):
             nc.vector.tensor_reduce(
-                out=sums[:, :, c, :],
-                in_=zh[c][:].rearrange("p t (g s) -> p t g s", s=PAGE), axis=AX.X, op=ALU.add)
+                out=sums[:, c, :, :],
+                in_=zh[c][:].rearrange("p t (g s) -> p g t s", s=PAGE), axis=AX.X, op=ALU.add)
         qg_codes = sb("qg_codes", [P, 2 * Q], U32)
         qg_scales = sb("qg_scales", [P, 2 * Q], U8)
-        nc.vector.scalar_tensor_tensor(
-            out=shift[:].rearrange("p t c g -> p t (c g)"), in0=sums[:].rearrange("p t c g -> p t (c g)"),
-            scalar=1.0 / PAGE, in1=share_sb[:].unsqueeze(2).to_broadcast([P, PACK, CHUNKS * PAGES]),
-            op0=ALU.mult, op1=ALU.mult)
         nc.vector.quantize_mx(out=qg_codes[:].bitcast(FP8X4), scales=qg_scales[:],
                               in_=qg_bf[:].rearrange("p n c j -> p (n c j)"))
-        for c in range(CHUNKS):
-            centre(c)
-        scale(nc.gpsimd, 0)
-        scale(nc.gpsimd, 1)
-        keys_sg = keep.tile([P, SLOTS], U8, name="keys_sg", tag="shift", align_bytes=64)
+        nc.vector.scalar_tensor_tensor(
+            out=shift[:].rearrange("p c g t -> p (c g) t"), in0=sums[:].rearrange("p c g t -> p (c g) t"),
+            scalar=1.0 / PAGE, in1=share_sb[:].unsqueeze(1).to_broadcast([P, CHUNKS * PAGES, PACK]),
+            op0=ALU.mult, op1=ALU.mult)
+        keys_sg = keep.tile([P, SLOTS], U8, name="keys_sg", tag="sums", align_bytes=64)
         nc.vector.tensor_copy(out=keys_sg[:], in_=keys_s[:].indirect(offsets[:]))
         a = psum.tile([P, SLOTS], F32, name="a")
         nc.tensor.matmul_mx(out=a[:], lhsT=qg_codes[:, :Q].bitcast(FP8X4), lhsT_scale=qg_scales[:, :Q],
                             rhs=keys_wg[:].bitcast(FP4X4), rhs_scale=keys_sg[:], start=True, stop=True)
-        scale(nc.vector, 2)
+        for c in range(CHUNKS):
+            centre(c)
+        scale(nc.gpsimd, 0, 0, CHUNK)
+        scale(nc.gpsimd, 1, 0, CHUNK // 2)
         neg_max = sb("neg_max", [P, 1], F32)
         nc.vector.tensor_reduce(out=neg_max[:], in_=a[:], axis=AX.X, op=ALU.max, negate=True)
         p = sb("p", [P, SLOTS], F32)
         z = sb("z", [P, 1], F32)
         nc.scalar.activation(out=p[:], in_=a[:], func=ACT.Exp, bias=neg_max[:], accum_out=z[:])
-        scale(nc.vector, 3)
+        z_pair = sb("z_pair", [P, 2], F32)
+        nc.scalar.mul(out=z_pair[:, 0:1], in_=z[:], mul=1.0 / 512.0)
+        nc.scalar.mul(out=z_pair[:, 1:2], in_=z[:], mul=-1.0)
+        scale(nc.vector, 1, CHUNK // 2, CHUNK)
+        scale(nc.vector, 2, 0, CHUNK)
+        scale(nc.vector, 3, 0, CHUNK)
         second_product(0)
         second_product(1)
-        rz = sb("rz", [P, 1], F32)
-        nc.vector.reciprocal(out=rz[:], in_=z[:])
-        rz_gain = sb("rz_gain", [P, 1], F32)
-        nc.vector.tensor_scalar_mul(out=rz_gain[:], in0=rz[:], scalar1=512.0)
-        rz_neg = sb("rz_neg", [P, 1], F32)
-        nc.vector.tensor_scalar_mul(out=rz_neg[:], in0=rz[:], scalar1=-1.0)
+        rz = sb("rz", [P, 2], F32)
+        nc.vector.reciprocal(out=rz[:], in_=z_pair[:])
 
         u = sb("u", [P, SLOTS], F32)
         total = sb("total", [P, 1], F32)
-        nc.vector.scalar_tensor_tensor(out=u[:], in0=c0[:], scalar=rz_gain[:], in1=p[:],
+        nc.vector.scalar_tensor_tensor(out=u[:], in0=c0[:], scalar=rz[:, 0:1], in1=p[:],
                                        op0=ALU.mult, op1=ALU.mult, accum_out=total[:])
         w = sb("w", [P, SLOTS], F32)
-        nc.vector.tensor_scalar(out=w[:], in0=p[:], scalar1=total[:], scalar2=rz_neg[:], op0=ALU.mult, op1=ALU.mult)
+        nc.vector.tensor_scalar(out=w[:], in0=p[:], scalar1=total[:], scalar2=rz[:, 1:2], op0=ALU.mult, op1=ALU.mult)
         nc.vector.tensor_tensor(out=gf[:].indirect(offsets[:]), in0=u[:], in1=w[:], op=ALU.add)
 
         edges = (0, 256, 768, 1280, 1792, 2048)

@@ -16,14 +16,21 @@ AX = mybir.AxisListType
 
 P = 128
 PACK = 4
+CONTRACTION = P * PACK
 R, T, SLOTS, Q = 512, 2048, 512, 128
+SCALE_ROWS = CONTRACTION // 32
+QUADRANT = 32
+GAIN = 512.0
 PAGE = 16
 CHUNK = 128
 CHUNKS = SLOTS // CHUNK
 PAGES = CHUNK // PAGE
-OUT_CHUNK = 512
+HALF_M = P // 2
+SCALAR_M = 16
+GPSIMD_SLOTS = 32
+OUT_EDGES = (0, 256, 768, 1280, 1792, 2048)
 
-FLOPS = 2 * 512 * SLOTS * (Q + R + Q)
+FLOPS = 2 * CONTRACTION * SLOTS * (Q + R + Q)
 
 
 def tile_attend_blrcentred_soft_kernel(tc, query, keys_words, keys_scales, tab_words, tab_scales,
@@ -33,8 +40,8 @@ def tile_attend_blrcentred_soft_kernel(tc, query, keys_words, keys_scales, tab_w
         keep = ctx.enter_context(tc.tile_pool(name="keep", bufs=1))
         psum = ctx.enter_context(tc.psum_pool(name="psum", bufs=1))
 
-        def sb(name, shape, dtype):
-            return keep.tile(shape, dtype, name=name, align_bytes=64)
+        def sb(name, shape, dtype, tag=None):
+            return keep.tile(shape, dtype, name=name, tag=tag or name, align_bytes=64)
 
         offsets = keep.tile([P, SLOTS // 16], U16, name="offsets")
         tab_w = sb("tab_w", [P, T], U16)
@@ -42,13 +49,9 @@ def tile_attend_blrcentred_soft_kernel(tc, query, keys_words, keys_scales, tab_w
         keys_w = sb("keys_w", [P, T], U16)
         keys_s = sb("keys_s", [P, T], U8)
         gf = sb("gf", [P, T], F32)
-        warm = sb("warm", [P, 1], F32)
-        warm2 = sb("warm2", [P, 1], F32)
 
         nc.vector.memset(tab_s[:].bitcast(I32), 0)
         nc.vector.memset(keys_s[:].bitcast(I32), 0)
-        nc.gpsimd.memset(warm[:], 0.0)
-        nc.scalar.activation(out=warm2[:], in_=warm[:], func=ACT.Exp)
         nc.vector.memset(gf[:], 0.0)
 
         def load_words(tile, words):
@@ -56,149 +59,145 @@ def tile_attend_blrcentred_soft_kernel(tc, query, keys_words, keys_scales, tab_w
 
         def load_scales(tile, scales):
             for f in range(4):
-                nc.sync.dma_start(out=tile[f : P : 32, :].bitcast(I32), in_=scales[0, f : 16 : 4, :].bitcast(I32))
+                nc.sync.dma_start(out=tile[f:P:QUADRANT, :].bitcast(I32),
+                                  in_=scales[0, f:SCALE_ROWS:4, :].bitcast(I32))
+
+        def load_rows(name, rows):
+            tile = sb(name, [P, PACK, rows.shape[1]], F32)
+            nc.sync.dma_start(out=tile[:], in_=rows.rearrange("(p j) c -> p j c", j=PACK))
+            return tile
+
+        def load_factors(name, vector):
+            tile = sb(name, [P, PACK], F32)
+            nc.sync.dma_start(out=tile[:], in_=vector.rearrange("(p t) o -> p (t o)", t=PACK))
+            return tile
 
         nc.sync.dma_start(offsets[:], offs)
         load_words(tab_w, tab_words)
         load_scales(tab_s, tab_scales)
-        w_rows = w1.rearrange("(p j) c -> p j c", j=PACK)
-        w_raw = []
-        for h in range(2):
-            half = sb("w_raw%d" % h, [P, PACK, R // 2], F32)
-            nc.sync.dma_start(out=half[:], in_=w_rows[:, :, h * (R // 2) : (h + 1) * (R // 2)])
-            w_raw.append(half)
+        w_raw = [load_rows("w_raw%d" % h, w1[:, h * (R // 2) : (h + 1) * (R // 2)]) for h in range(2)]
         load_words(keys_w, keys_words)
+        share_sb = load_factors("share_sb", share)
+        q_raw = load_rows("q_raw", query)
+        g_raw = load_rows("g_raw", gout)
         load_scales(keys_s, keys_scales)
-        share_sb = sb("share_sb", [P, PACK], F32)
-        nc.gpsimd.dma_start(out=share_sb[:], in_=share.rearrange("(p t) o -> p (t o)", t=PACK))
-        hsc_sb = sb("hsc_sb", [P, PACK], F32)
-        nc.gpsimd.dma_start(out=hsc_sb[:], in_=hsc.rearrange("(p t) o -> p (t o)", t=PACK))
-        q_raw = sb("q_raw", [P, PACK, Q], F32)
-        nc.sync.dma_start(out=q_raw[:], in_=query.rearrange("(p j) c -> p j c", j=PACK))
-        g_raw = sb("g_raw", [P, PACK, Q], F32)
-        nc.sync.dma_start(out=g_raw[:], in_=gout.rearrange("(p j) c -> p j c", j=PACK))
+        hsc_sb = load_factors("hsc_sb", hsc)
         old_sb = sb("old_sb", [P, T], F32)
         nc.sync.dma_start(out=old_sb[:], in_=old)
 
-        def gather(name, window, dtype):
-            got = sb(name, [P, SLOTS], dtype)
+        def gather(name, window, dtype, tag=None):
+            got = sb(name, [P, SLOTS], dtype, tag)
             nc.vector.tensor_copy(out=got[:], in_=window[:].indirect(offsets[:]))
             return got
 
+        def quantise(codes, scales, values):
+            nc.vector.quantize_mx(out=codes.bitcast(FP8X4), scales=scales, in_=values)
+
+        def product(result, codes, scales, moving, moving_scales):
+            nc.tensor.matmul_mx(out=result, lhsT=codes.bitcast(FP8X4), lhsT_scale=scales,
+                                rhs=moving, rhs_scale=moving_scales, start=True, stop=True)
+
         tab_wg = gather("tab_wg", tab_w, U16)
         tab_sg = gather("tab_sg", tab_s, U8)
-
         w_bf = sb("w_bf", [P, PACK, P, PACK], BF16)
-        for copy, h, lo, hi in ((nc.scalar.copy, 0, 0, 64), (nc.scalar.copy, 1, 0, 24), (nc.vector.tensor_copy, 1, 24, 64)):
-            copy(out=w_bf[:, :, h * 64 + lo : h * 64 + hi, :].rearrange("p t m j -> p m j t"),
-                 in_=w_raw[h][:].rearrange("p j (m t) -> p m j t", t=PACK)[:, lo:hi, :, :])
+        for copy, h, lo, hi in ((nc.scalar.copy, 0, 0, HALF_M), (nc.scalar.copy, 1, 0, SCALAR_M),
+                                (nc.vector.tensor_copy, 1, SCALAR_M, HALF_M)):
+            for t in (0, 2):
+                copy(out=w_bf[:, t : t + 2, h * HALF_M + lo : h * HALF_M + hi, :].rearrange("p t m j -> p m j t"),
+                     in_=w_raw[h][:].rearrange("p j (m t) -> p m j t", t=PACK)[:, lo:hi, :, t : t + 2])
         w_codes = sb("w_codes", [P, R], U32)
         w_scales = sb("w_scales", [P, R], U8)
-        nc.vector.quantize_mx(out=w_codes[:].bitcast(FP8X4), scales=w_scales[:],
-                              in_=w_bf[:].rearrange("p t m j -> p (t m j)"))
+        quantise(w_codes[:], w_scales[:], w_bf[:].rearrange("p t m j -> p (t m j)"))
 
         qg_bf = sb("qg_bf", [P, 2, Q, PACK], BF16)
         for n, raw in enumerate((q_raw, g_raw)):
-            nc.scalar.copy(
-                out=qg_bf[:, n, :, :].rearrange("p (c i) j -> p c j i", i=4),
-                in_=raw[:].rearrange("p j (c i) -> p c j i", i=4))
+            nc.scalar.copy(out=qg_bf[:, n, :, :].rearrange("p (c i) j -> p c j i", i=4),
+                           in_=raw[:].rearrange("p j (c i) -> p c j i", i=4))
 
         zh = []
         for c in range(CHUNKS):
             bank = psum.tile([P, PACK, CHUNK], F32, name="zh%d" % c)
             cols = slice(c * CHUNK, (c + 1) * CHUNK)
             for t in range(PACK):
-                nc.tensor.matmul_mx(
-                    out=bank[:, t, :],
-                    lhsT=w_codes[:, t * P : (t + 1) * P].bitcast(FP8X4),
-                    lhsT_scale=w_scales[:, t * P : (t + 1) * P],
-                    rhs=tab_wg[:, cols].bitcast(FP4X4), rhs_scale=tab_sg[:, cols],
-                    start=True, stop=True)
+                tile_t = slice(t * P, (t + 1) * P)
+                product(bank[:, t, :], w_codes[:, tile_t], w_scales[:, tile_t],
+                        tab_wg[:, cols].bitcast(FP4X4), tab_sg[:, cols])
             zh.append(bank)
 
-        sums = keep.tile([P, CHUNKS, PAGES, PACK], F32, name="sums", tag="sums", align_bytes=64)
-        shift = sb("shift", [P, CHUNKS, PAGES, PACK], F32)
-        hs_bf = [sb("hs_bf%d" % n, [P, 2, CHUNK, PACK], BF16) for n in range(2)]
-        hs_codes = sb("hs_codes", [P, SLOTS], U32)
-        hs_scales = sb("hs_scales", [P, SLOTS], U8)
-        hv = {}
+        keys_wg = gather("keys_wg", keys_w, U16, tag="w_bf")
 
-        def centre(c):
-            x = sb("x%d" % c, [P, CHUNK, PACK], F32)
-            nc.vector.tensor_tensor(
-                out=x[:].rearrange("p (g s) t -> p g s t", s=PAGE),
-                in0=zh[c][:].rearrange("p t (g s) -> p g s t", s=PAGE),
-                in1=shift[:, c, :, :].unsqueeze(2).to_broadcast([P, PAGES, PAGE, PACK]),
-                op=ALU.subtract)
-            hv[c] = sb("hv%d" % c, [P, CHUNK, PACK], F32)
-            nc.scalar.activation(out=hv[c][:], in_=x[:], func=ACT.Tanh)
-
-        def scale(engine, c, lo, hi):
-            engine.tensor_tensor(
-                out=hs_bf[c // 2][:, c % 2, lo:hi, :], in0=hv[c][:, lo:hi, :],
-                in1=hsc_sb[:].unsqueeze(1).to_broadcast([P, hi - lo, PACK]), op=ALU.mult)
-
-        c0 = psum.tile([P, SLOTS], F32, name="c0")
-
-        def second_product(n):
-            cols = slice(2 * n * CHUNK, 2 * (n + 1) * CHUNK)
-            nc.vector.quantize_mx(out=hs_codes[:, cols].bitcast(FP8X4), scales=hs_scales[:, cols],
-                                  in_=hs_bf[n][:].rearrange("p c i t -> p (c i t)"))
-            nc.tensor.matmul_mx(out=c0[:, cols], lhsT=qg_codes[:, Q:].bitcast(FP8X4), lhsT_scale=qg_scales[:, Q:],
-                                rhs=hs_codes[:, cols].bitcast(FP8X4), rhs_scale=hs_scales[:, cols],
-                                start=True, stop=True)
-
-
-        keys_wg = gather("keys_wg", keys_w, U16)
+        sums = sb("sums", [P, CHUNKS, PAGES, PACK], F32)
         for c in range(CHUNKS):
-            nc.vector.tensor_reduce(
-                out=sums[:, c, :, :],
-                in_=zh[c][:].rearrange("p t (g s) -> p g t s", s=PAGE), axis=AX.X, op=ALU.add)
+            nc.vector.tensor_reduce(out=sums[:, c, :, :], in_=zh[c][:].rearrange("p t (g s) -> p g t s", s=PAGE),
+                                    axis=AX.X, op=ALU.add)
         qg_codes = sb("qg_codes", [P, 2 * Q], U32)
         qg_scales = sb("qg_scales", [P, 2 * Q], U8)
-        nc.vector.quantize_mx(out=qg_codes[:].bitcast(FP8X4), scales=qg_scales[:],
-                              in_=qg_bf[:].rearrange("p n c j -> p (n c j)"))
+        quantise(qg_codes[:], qg_scales[:], qg_bf[:].rearrange("p n c j -> p (n c j)"))
+        shift = sb("shift", [P, CHUNKS, PAGES, PACK], F32)
         nc.vector.scalar_tensor_tensor(
             out=shift[:].rearrange("p c g t -> p (c g) t"), in0=sums[:].rearrange("p c g t -> p (c g) t"),
             scalar=1.0 / PAGE, in1=share_sb[:].unsqueeze(1).to_broadcast([P, CHUNKS * PAGES, PACK]),
             op0=ALU.mult, op1=ALU.mult)
-        keys_sg = keep.tile([P, SLOTS], U8, name="keys_sg", tag="sums", align_bytes=64)
-        nc.vector.tensor_copy(out=keys_sg[:], in_=keys_s[:].indirect(offsets[:]))
+
+        keys_sg = gather("keys_sg", keys_s, U8, tag="sums")
         a = psum.tile([P, SLOTS], F32, name="a")
-        nc.tensor.matmul_mx(out=a[:], lhsT=qg_codes[:, :Q].bitcast(FP8X4), lhsT_scale=qg_scales[:, :Q],
-                            rhs=keys_wg[:].bitcast(FP4X4), rhs_scale=keys_sg[:], start=True, stop=True)
+        product(a[:], qg_codes[:, :Q], qg_scales[:, :Q], keys_wg[:].bitcast(FP4X4), keys_sg[:])
+
+        hv = []
         for c in range(CHUNKS):
-            centre(c)
+            centred = sb("centred%d" % c, [P, CHUNK, PACK], F32)
+            nc.vector.tensor_tensor(
+                out=centred[:].rearrange("p (g s) t -> p g s t", s=PAGE),
+                in0=zh[c][:].rearrange("p t (g s) -> p g s t", s=PAGE),
+                in1=shift[:, c, :, :].unsqueeze(2).to_broadcast([P, PAGES, PAGE, PACK]),
+                op=ALU.subtract)
+            hv.append(sb("hv%d" % c, [P, CHUNK, PACK], F32))
+            nc.scalar.activation(out=hv[c][:], in_=centred[:], func=ACT.Tanh)
+
+        hs_bf = [sb("hs_bf%d" % n, [P, 2, CHUNK, PACK], BF16) for n in range(CHUNKS // 2)]
+
+        def scale(engine, c, lo, hi):
+            engine.tensor_tensor(out=hs_bf[c // 2][:, c % 2, lo:hi, :], in0=hv[c][:, lo:hi, :],
+                                 in1=hsc_sb[:].unsqueeze(1).to_broadcast([P, hi - lo, PACK]), op=ALU.mult)
+
         scale(nc.gpsimd, 0, 0, CHUNK)
-        scale(nc.gpsimd, 1, 0, CHUNK // 2)
+        scale(nc.gpsimd, 1, 0, GPSIMD_SLOTS)
+
         neg_max = sb("neg_max", [P, 1], F32)
         nc.vector.tensor_reduce(out=neg_max[:], in_=a[:], axis=AX.X, op=ALU.max, negate=True)
-        p = sb("p", [P, SLOTS], F32)
+        weights = sb("weights", [P, SLOTS], F32)
         z = sb("z", [P, 1], F32)
-        nc.scalar.activation(out=p[:], in_=a[:], func=ACT.Exp, bias=neg_max[:], accum_out=z[:])
+        nc.scalar.activation(out=weights[:], in_=a[:], func=ACT.Exp, bias=neg_max[:], accum_out=z[:])
         z_pair = sb("z_pair", [P, 2], F32)
-        nc.scalar.mul(out=z_pair[:, 0:1], in_=z[:], mul=1.0 / 512.0)
+        nc.scalar.mul(out=z_pair[:, 0:1], in_=z[:], mul=1.0 / GAIN)
         nc.scalar.mul(out=z_pair[:, 1:2], in_=z[:], mul=-1.0)
-        scale(nc.vector, 1, CHUNK // 2, CHUNK)
-        scale(nc.vector, 2, 0, CHUNK)
-        scale(nc.vector, 3, 0, CHUNK)
-        second_product(0)
-        second_product(1)
-        rz = sb("rz", [P, 2], F32)
-        nc.vector.reciprocal(out=rz[:], in_=z_pair[:])
 
-        u = sb("u", [P, SLOTS], F32)
+        scale(nc.vector, 1, GPSIMD_SLOTS, CHUNK)
+        for c in range(2, CHUNKS):
+            scale(nc.vector, c, 0, CHUNK)
+
+        hs_codes = sb("hs_codes", [P, SLOTS], U32)
+        hs_scales = sb("hs_scales", [P, SLOTS], U8)
+        c0 = psum.tile([P, SLOTS], F32, name="c0")
+        for n in range(CHUNKS // 2):
+            cols = slice(2 * n * CHUNK, 2 * (n + 1) * CHUNK)
+            quantise(hs_codes[:, cols], hs_scales[:, cols], hs_bf[n][:].rearrange("p c s t -> p (c s t)"))
+            product(c0[:, cols], qg_codes[:, Q:], qg_scales[:, Q:], hs_codes[:, cols].bitcast(FP8X4), hs_scales[:, cols])
+
+        inverse = sb("inverse", [P, 2], F32)
+        nc.vector.reciprocal(out=inverse[:], in_=z_pair[:])
+        direct = sb("direct", [P, SLOTS], F32)
         total = sb("total", [P, 1], F32)
-        nc.vector.scalar_tensor_tensor(out=u[:], in0=c0[:], scalar=rz[:, 0:1], in1=p[:],
+        nc.vector.scalar_tensor_tensor(out=direct[:], in0=c0[:], scalar=inverse[:, 0:1], in1=weights[:],
                                        op0=ALU.mult, op1=ALU.mult, accum_out=total[:])
-        w = sb("w", [P, SLOTS], F32)
-        nc.vector.tensor_scalar(out=w[:], in0=p[:], scalar1=total[:], scalar2=rz[:, 1:2], op0=ALU.mult, op1=ALU.mult)
-        nc.vector.tensor_tensor(out=gf[:].indirect(offsets[:]), in0=u[:], in1=w[:], op=ALU.add)
+        through_sum = sb("through_sum", [P, SLOTS], F32)
+        nc.vector.tensor_scalar(out=through_sum[:], in0=weights[:], scalar1=total[:], scalar2=inverse[:, 1:2],
+                                op0=ALU.mult, op1=ALU.mult)
+        nc.vector.tensor_tensor(out=gf[:].indirect(offsets[:]), in0=direct[:], in1=through_sum[:], op=ALU.add)
 
-        edges = (0, 256, 768, 1280, 1792, 2048)
-        for n in range(len(edges) - 1):
-            cols = slice(edges[n], edges[n + 1])
-            y = sb("y%d" % n, [P, edges[n + 1] - edges[n]], F32)
+        for n in range(len(OUT_EDGES) - 1):
+            cols = slice(OUT_EDGES[n], OUT_EDGES[n + 1])
+            y = sb("y%d" % n, [P, OUT_EDGES[n + 1] - OUT_EDGES[n]], F32)
             nc.vector.tensor_tensor(out=y[:], in0=gf[:, cols], in1=old_sb[:, cols], op=ALU.add)
             queue = nc.sync if n % 2 == 0 else nc.scalar
             queue.dma_start(out=out[:, cols], in_=y[:])

from contextlib import ExitStack

import concourse.mybir as mybir

F32 = mybir.dt.float32
BF16 = mybir.dt.bfloat16
I32 = mybir.dt.int32
U32 = mybir.dt.uint32
U16 = mybir.dt.uint16
U8 = mybir.dt.uint8
FP8X4 = mybir.dt.float8_e4m3fn_x4
FP4X4 = mybir.dt.float4_e2m1fn_x4
ALU = mybir.AluOpType
ACT = mybir.ActivationFunctionType
AX = mybir.AxisListType

P = 128
PACK = 4
CONTRACTION = P * PACK
R, T, SLOTS, Q = 512, 2048, 512, 128
SCALE_ROWS = CONTRACTION // 32
QUADRANT = 32
GAIN = 512.0
PAGE = 16
CHUNK = 128
CHUNKS = SLOTS // CHUNK
PAGES = CHUNK // PAGE
HALF_M = P // 2
SCALAR_M = 16
GPSIMD_SLOTS = 32
OUT_EDGES = (0, 256, 768, 1280, 1792, 2048)

FLOPS = 2 * CONTRACTION * SLOTS * (Q + R + Q)


def tile_attend_blrcentred_soft_kernel(tc, query, keys_words, keys_scales, tab_words, tab_scales,
                                        w1, share, gout, hsc, old, offs, out):
    nc = tc.nc
    with ExitStack() as ctx:
        keep = ctx.enter_context(tc.tile_pool(name="keep", bufs=1))
        psum = ctx.enter_context(tc.psum_pool(name="psum", bufs=1))

        def sb(name, shape, dtype, tag=None):
            return keep.tile(shape, dtype, name=name, tag=tag or name, align_bytes=64)

        offsets = keep.tile([P, SLOTS // 16], U16, name="offsets")
        tab_w = sb("tab_w", [P, T], U16)
        tab_s = sb("tab_s", [P, T], U8)
        keys_w = sb("keys_w", [P, T], U16)
        keys_s = sb("keys_s", [P, T], U8)
        gf = sb("gf", [P, T], F32)

        nc.vector.memset(tab_s[:].bitcast(I32), 0)
        nc.vector.memset(keys_s[:].bitcast(I32), 0)
        nc.vector.memset(gf[:], 0.0)

        def load_words(tile, words):
            nc.sync.dma_start(out=tile[:].bitcast(I32), in_=words[0].bitcast(I32))

        def load_scales(tile, scales):
            for f in range(4):
                nc.sync.dma_start(out=tile[f:P:QUADRANT, :].bitcast(I32),
                                  in_=scales[0, f:SCALE_ROWS:4, :].bitcast(I32))

        def load_rows(name, rows):
            tile = sb(name, [P, PACK, rows.shape[1]], F32)
            nc.sync.dma_start(out=tile[:], in_=rows.rearrange("(p j) c -> p j c", j=PACK))
            return tile

        def load_factors(name, vector):
            tile = sb(name, [P, PACK], F32)
            nc.sync.dma_start(out=tile[:], in_=vector.rearrange("(p t) o -> p (t o)", t=PACK))
            return tile

        nc.sync.dma_start(offsets[:], offs)
        load_words(tab_w, tab_words)
        load_scales(tab_s, tab_scales)
        w_raw = [load_rows("w_raw%d" % h, w1[:, h * (R // 2) : (h + 1) * (R // 2)]) for h in range(2)]
        load_words(keys_w, keys_words)
        share_sb = load_factors("share_sb", share)
        q_raw = load_rows("q_raw", query)
        g_raw = load_rows("g_raw", gout)
        load_scales(keys_s, keys_scales)
        hsc_sb = load_factors("hsc_sb", hsc)
        old_sb = sb("old_sb", [P, T], F32)
        nc.sync.dma_start(out=old_sb[:], in_=old)

        def gather(name, window, dtype, tag=None):
            got = sb(name, [P, SLOTS], dtype, tag)
            nc.vector.tensor_copy(out=got[:], in_=window[:].indirect(offsets[:]))
            return got

        def quantise(codes, scales, values):
            nc.vector.quantize_mx(out=codes.bitcast(FP8X4), scales=scales, in_=values)

        def product(result, codes, scales, moving, moving_scales):
            nc.tensor.matmul_mx(out=result, lhsT=codes.bitcast(FP8X4), lhsT_scale=scales,
                                rhs=moving, rhs_scale=moving_scales, start=True, stop=True)

        tab_wg = gather("tab_wg", tab_w, U16)
        tab_sg = gather("tab_sg", tab_s, U8)
        w_bf = sb("w_bf", [P, PACK, P, PACK], BF16)
        for copy, h, lo, hi in ((nc.scalar.copy, 0, 0, HALF_M), (nc.scalar.copy, 1, 0, SCALAR_M),
                                (nc.vector.tensor_copy, 1, SCALAR_M, HALF_M)):
            for t in (0, 2):
                copy(out=w_bf[:, t : t + 2, h * HALF_M + lo : h * HALF_M + hi, :].rearrange("p t m j -> p m j t"),
                     in_=w_raw[h][:].rearrange("p j (m t) -> p m j t", t=PACK)[:, lo:hi, :, t : t + 2])
        w_codes = sb("w_codes", [P, R], U32)
        w_scales = sb("w_scales", [P, R], U8)
        quantise(w_codes[:], w_scales[:], w_bf[:].rearrange("p t m j -> p (t m j)"))

        qg_bf = sb("qg_bf", [P, 2, Q, PACK], BF16)
        for n, raw in enumerate((q_raw, g_raw)):
            nc.scalar.copy(out=qg_bf[:, n, :, :].rearrange("p (c i) j -> p c j i", i=4),
                           in_=raw[:].rearrange("p j (c i) -> p c j i", i=4))

        zh = []
        for c in range(CHUNKS):
            bank = psum.tile([P, PACK, CHUNK], F32, name="zh%d" % c)
            cols = slice(c * CHUNK, (c + 1) * CHUNK)
            for t in range(PACK):
                tile_t = slice(t * P, (t + 1) * P)
                product(bank[:, t, :], w_codes[:, tile_t], w_scales[:, tile_t],
                        tab_wg[:, cols].bitcast(FP4X4), tab_sg[:, cols])
            zh.append(bank)

        keys_wg = gather("keys_wg", keys_w, U16, tag="w_bf")

        sums = sb("sums", [P, CHUNKS, PAGES, PACK], F32)
        for c in range(CHUNKS):
            nc.vector.tensor_reduce(out=sums[:, c, :, :], in_=zh[c][:].rearrange("p t (g s) -> p g t s", s=PAGE),
                                    axis=AX.X, op=ALU.add)
        qg_codes = sb("qg_codes", [P, 2 * Q], U32)
        qg_scales = sb("qg_scales", [P, 2 * Q], U8)
        quantise(qg_codes[:], qg_scales[:], qg_bf[:].rearrange("p n c j -> p (n c j)"))
        shift = sb("shift", [P, CHUNKS, PAGES, PACK], F32)
        nc.vector.scalar_tensor_tensor(
            out=shift[:].rearrange("p c g t -> p (c g) t"), in0=sums[:].rearrange("p c g t -> p (c g) t"),
            scalar=1.0 / PAGE, in1=share_sb[:].unsqueeze(1).to_broadcast([P, CHUNKS * PAGES, PACK]),
            op0=ALU.mult, op1=ALU.mult)

        keys_sg = gather("keys_sg", keys_s, U8, tag="sums")
        a = psum.tile([P, SLOTS], F32, name="a")
        product(a[:], qg_codes[:, :Q], qg_scales[:, :Q], keys_wg[:].bitcast(FP4X4), keys_sg[:])

        hv = []
        for c in range(CHUNKS):
            centred = sb("centred%d" % c, [P, CHUNK, PACK], F32)
            nc.vector.tensor_tensor(
                out=centred[:].rearrange("p (g s) t -> p g s t", s=PAGE),
                in0=zh[c][:].rearrange("p t (g s) -> p g s t", s=PAGE),
                in1=shift[:, c, :, :].unsqueeze(2).to_broadcast([P, PAGES, PAGE, PACK]),
                op=ALU.subtract)
            hv.append(sb("hv%d" % c, [P, CHUNK, PACK], F32))
            nc.scalar.activation(out=hv[c][:], in_=centred[:], func=ACT.Tanh)

        hs_bf = [sb("hs_bf%d" % n, [P, 2, CHUNK, PACK], BF16) for n in range(CHUNKS // 2)]

        def scale(engine, c, lo, hi):
            engine.tensor_tensor(out=hs_bf[c // 2][:, c % 2, lo:hi, :], in0=hv[c][:, lo:hi, :],
                                 in1=hsc_sb[:].unsqueeze(1).to_broadcast([P, hi - lo, PACK]), op=ALU.mult)

        scale(nc.gpsimd, 0, 0, CHUNK)
        scale(nc.gpsimd, 1, 0, GPSIMD_SLOTS)

        neg_max = sb("neg_max", [P, 1], F32)
        nc.vector.tensor_reduce(out=neg_max[:], in_=a[:], axis=AX.X, op=ALU.max, negate=True)
        weights = sb("weights", [P, SLOTS], F32)
        z = sb("z", [P, 1], F32)
        nc.scalar.activation(out=weights[:], in_=a[:], func=ACT.Exp, bias=neg_max[:], accum_out=z[:])
        z_pair = sb("z_pair", [P, 2], F32)
        nc.scalar.mul(out=z_pair[:, 0:1], in_=z[:], mul=1.0 / GAIN)
        nc.scalar.mul(out=z_pair[:, 1:2], in_=z[:], mul=-1.0)

        scale(nc.vector, 1, GPSIMD_SLOTS, CHUNK)
        for c in range(2, CHUNKS):
            scale(nc.vector, c, 0, CHUNK)

        hs_codes = sb("hs_codes", [P, SLOTS], U32)
        hs_scales = sb("hs_scales", [P, SLOTS], U8)
        c0 = psum.tile([P, SLOTS], F32, name="c0")
        for n in range(CHUNKS // 2):
            cols = slice(2 * n * CHUNK, 2 * (n + 1) * CHUNK)
            quantise(hs_codes[:, cols], hs_scales[:, cols], hs_bf[n][:].rearrange("p c s t -> p (c s t)"))
            product(c0[:, cols], qg_codes[:, Q:], qg_scales[:, Q:], hs_codes[:, cols].bitcast(FP8X4), hs_scales[:, cols])

        inverse = sb("inverse", [P, 2], F32)
        nc.vector.reciprocal(out=inverse[:], in_=z_pair[:])
        direct = sb("direct", [P, SLOTS], F32)
        total = sb("total", [P, 1], F32)
        nc.vector.scalar_tensor_tensor(out=direct[:], in0=c0[:], scalar=inverse[:, 0:1], in1=weights[:],
                                       op0=ALU.mult, op1=ALU.mult, accum_out=total[:])
        through_sum = sb("through_sum", [P, SLOTS], F32)
        nc.vector.tensor_scalar(out=through_sum[:], in0=weights[:], scalar1=total[:], scalar2=inverse[:, 1:2],
                                op0=ALU.mult, op1=ALU.mult)
        nc.vector.tensor_tensor(out=gf[:].indirect(offsets[:]), in0=direct[:], in1=through_sum[:], op=ALU.add)

        for n in range(len(OUT_EDGES) - 1):
            cols = slice(OUT_EDGES[n], OUT_EDGES[n + 1])
            y = sb("y%d" % n, [P, OUT_EDGES[n + 1] - OUT_EDGES[n]], F32)
            nc.vector.tensor_tensor(out=y[:], in0=gf[:, cols], in1=old_sb[:, cols], op=ALU.add)
            queue = nc.sync if n % 2 == 0 else nc.scalar
            queue.dma_start(out=out[:, cols], in_=y[:])
